import numpy as np
import ml_dtypes


def mxq(x, axis, fmt="e4m3"):
    dtype, down = {"e4m3": (ml_dtypes.float8_e4m3fn, 7), "e5m2": (ml_dtypes.float8_e5m2, 14)}[fmt]
    v = np.moveaxis(np.asarray(x, np.float32).astype(ml_dtypes.bfloat16).astype(np.float64), axis, -1)
    blocks = v.reshape(v.shape[:-1] + (-1, 32))
    amax = np.abs(blocks).max(-1, keepdims=True)
    byte = np.maximum(np.where(amax > 0, np.frexp(amax)[1] - 1 + 127, 0) - down, 1)
    scale = np.exp2(byte - 127.0)
    codes = (blocks / scale).astype(np.float32).astype(dtype).astype(np.float64)
    return np.moveaxis((codes * scale).reshape(v.shape), -1, axis)


WIDE = False


def mx_kscale(k):
    if not WIDE:
        return np.ones(k)
    levels = np.array([10, -10, 5, -5, 0])
    if k % 512:
        return np.exp2(np.random.permutation(np.resize(levels, k // 32))).repeat(32)
    a = np.empty((k // 512, 16))
    for p in range(k // 512):
        a[p, :8] = np.random.permutation(np.resize(levels, 8))
        for g in range(8):
            far = levels[np.abs(levels - a[p, g]) >= 10]
            a[p, g + 8] = far[np.random.randint(len(far))]
    return np.exp2(a.ravel()).repeat(32)


def f64(x):
    return np.asarray(x).astype(np.float64)


def striped(idx):
    return np.tile(idx.reshape(-1, 16).T, (8, 1)).astype(np.uint16)


def unstriped(offs):
    return offs[:16].T.reshape(-1).astype(np.int64)


def pack_weight(w):
    k, n = w.shape
    w = f64(np.asarray(w, np.float32).astype(ml_dtypes.bfloat16)).reshape(k // 32, 32, n)
    amax = np.abs(w).max(1)
    byte = np.clip(np.where(amax > 0, np.frexp(amax)[1] - 1 + 127 - 7, 1), 1, 254)
    scaled = (w * np.exp2(127.0 - byte)[:, None, :]).reshape(k, n).astype(np.float32)
    words = np.ascontiguousarray(scaled.reshape(k // 512, 128, 4, n).transpose(0, 1, 3, 2)).astype(ml_dtypes.float8_e4m3fn).view(np.uint8)
    return words, np.ascontiguousarray(byte.astype(np.uint8).reshape(k // 512, 16, n))


def unpack_weight(words, scales):
    g, p, n, _ = words.shape
    vals = np.ascontiguousarray(words).view(ml_dtypes.float8_e4m3fn).astype(np.float64) * np.repeat(np.exp2(scales.astype(np.float64) - 127.0), 8, axis=1)[..., None]
    return vals.transpose(0, 1, 3, 2).reshape(g * 512, n)


K, T, S, J = 1536, 1024, 512, 512
P = 2 ** 7


def setup_inputs():
    n = np.random.standard_normal
    s = mx_kscale(K)[:, None]
    packed_xT = pack_weight(n((K, T)) * s)
    return {
        "x_words": packed_xT[0],
        "x_scales": packed_xT[1],
        "hT": (n((K, J)) / np.sqrt(K) / s).astype(np.float32),
        "norm2": (np.tile(0.5 * np.random.standard_normal(T), (P, 1))).astype(np.float32),
        "offs": striped(np.random.permutation(T)[:S]),
    }


def reference(x_words, x_scales, hT, norm2, offs):
    hTq = mxq(f64(hT), 0, "e4m3")
    xq = unpack_weight(x_words, x_scales)[:, unstriped(offs)]
    y = 2.0 * (hTq.T @ xq) - (f64(norm2)[:1][:, unstriped(offs)])
    e = np.exp(y - y.max(axis=1, keepdims=True))
    return e / e.sum(axis=1, keepdims=True)

@@ -1,0 +1,227 @@
+from contextlib import ExitStack
+
+import concourse.mybir as mybir
+from concourse.masks import make_identity
+
+K, T, S, J = 1536, 1024, 512, 512
+P = 128
+PASSES = 3
+F32 = mybir.dt.float32
+BF16 = mybir.dt.bfloat16
+U32 = mybir.dt.uint32
+I32 = mybir.dt.int32
+U16 = mybir.dt.uint16
+U8 = mybir.dt.uint8
+FP8X4 = mybir.dt.float8_e4m3fn_x4
+ALU = mybir.AluOpType
+ACT = mybir.ActivationFunctionType
+FLOPS = 2 * K * S * J
+
+
+def tile_picked_zcos_nca_p_kernel(tc, x_words, x_scales, hT, norm2, offs, out):
+    nc = tc.nc
+    with ExitStack() as ctx:
+        keep = ctx.enter_context(tc.tile_pool(name="keep", bufs=1))
+        psum = ctx.enter_context(tc.psum_pool(name="psum", bufs=1))
+
+        offsets = keep.tile([P, S // 16], U16, name="offsets")
+        nwin = keep.tile([P, T], F32, name="nwin")
+        swin = keep.tile([P, T], U8, name="swin", align_bytes=64)
+        wwin = [keep.tile([P, T], I32, name="wwin%d" % a, align_bytes=64) for a in range(PASSES)]
+        xw = [keep.tile([P, S], U32, name="xw%d" % a, align_bytes=64) for a in range(PASSES)]
+        xs = keep.tile([P, S], U8, name="xs", align_bytes=64)
+        ng = keep.tile([P, S], F32, name="ng")
+        ncol = keep.tile([P, 4], F32, name="ncol")
+        nb = keep.tile([P, S], F32, name="nb")
+        ident = keep.tile([P, P], F32, name="ident")
+        warm = keep.tile([P, 2], F32, name="warm")
+        acc = [psum.tile([P, S], F32, name="acc%d" % t) for t in range(4)]
+        nt = psum.tile([P, 4, P], F32, name="nt")
+        nbp = psum.tile([P, 4, P], F32, name="nbp")
+        raw, grouped, codes, scales, where = {}, {}, {}, {}, {}
+        z, e, zmin, ssum, rinv, o = {}, {}, {}, {}, {}, {}
+
+        def clear():
+            nc.gpsimd.memset(swin[:].bitcast(I32), 0)
+            nc.vector.memset(nwin[32:64, :], 0.0)
+            nc.vector.memset(nwin[64:128, :], 0.0)
+
+        def warm_exp():
+            nc.vector.memset(warm[:, 0:1], 0.0)
+            nc.scalar.activation(warm[:, 1:2], warm[:, 0:1], ACT.Exp)
+
+        def load_offs():
+            nc.sync.dma_start(offsets[:], offs)
+
+        def load_norm(eng):
+            eng.dma_start(nwin[0:32, :], norm2[0:32, :])
+
+        def load_scales(eng):
+            for q in range(4):
+                eng.dma_start(swin[32 * q : 32 * q + 12, :].bitcast(I32), x_scales[:, 4 * q : 4 * q + 4, :].bitcast(I32))
+
+        def load_words(a):
+            nc.sync.dma_start(wwin[a][:], x_words[a].rearrange("p n t -> p (n t)").bitcast(I32))
+
+        def load_h(a, t0, nt_):
+            w = nt_ * P
+            key = (a, t0)
+            raw[key] = keep.tile([P, 4, w], F32, name="raw%d_%d" % key)
+            grouped[key] = keep.tile([P, w, 4], BF16, name="grp%d_%d" % key, align_bytes=64)
+            codes[key] = keep.tile([P, w], U32, name="cod%d_%d" % key, align_bytes=64)
+            scales[key] = keep.tile([P, w], U8, name="scl%d_%d" % key, align_bytes=64)
+            for t in range(nt_):
+                where[(a, t0 + t)] = (key, t)
+            rows = hT[a * 512 : (a + 1) * 512, t0 * P : t0 * P + w]
+            nc.sync.dma_start(raw[key][:], rows.rearrange("(p j) w -> p j w", j=4))
+
+        def cast(eng, a, t0, c0, c1):
+            key = (a, t0)
+            dst = grouped[key][:, c0:c1, :].rearrange("p (c i) t -> p c t i", i=4)
+            src = raw[key][:, :, c0:c1].rearrange("p t (c i) -> p c t i", i=4)
+            if eng == "s":
+                nc.scalar.copy(dst, src)
+            elif eng == "v":
+                nc.vector.tensor_copy(dst, src)
+
+        def quant(a, t0, c0, c1):
+            key = (a, t0)
+            nc.vector.quantize_mx(
+                out=codes[key][:, c0:c1].bitcast(FP8X4),
+                scales=scales[key][:, c0:c1],
+                in_=grouped[key][:, c0:c1, :].rearrange("p w j -> p (w j)"),
+            )
+
+        def gather_words(a):
+            nc.vector.tensor_copy(xw[a][:], wwin[a][:].bitcast(U32).indirect(offsets[:]))
+
+        def gather_scales():
+            nc.vector.tensor_copy(xs[:], swin[:].indirect(offsets[:]))
+
+        def gather_norm():
+            nc.vector.tensor_copy(ng[:], nwin[:].indirect(offsets[:]))
+
+        def spread_norm():
+            for b in range(4):
+                nc.tensor.transpose(nt[:, b, :], ng[:, b * P : (b + 1) * P], ident[:])
+            nc.scalar.copy(ncol[:], nt[:, :, 0])
+            for b in range(4):
+                nc.tensor.transpose(nbp[:, b, :], ncol[:, b : b + 1].to_broadcast([P, P]), ident[:])
+            nc.scalar.copy(nb[:], nbp[:].rearrange("p b c -> p (b c)"))
+
+        def mm(a, t):
+            key, i = where[(a, t)]
+            cols = slice(i * P, (i + 1) * P)
+            nc.tensor.matmul_mx(
+                out=acc[t][:],
+                lhsT=codes[key][:, cols].bitcast(FP8X4),
+                lhsT_scale=scales[key][:, cols],
+                rhs=xw[a][:].bitcast(FP8X4),
+                rhs_scale=xs[4 * a : P, :],
+                start=(a == 0),
+                stop=(a == PASSES - 1),
+            )
+
+        def dist(t):
+            z[t] = keep.tile([P, S], F32, name="z%d" % t)
+            nc.vector.scalar_tensor_tensor(z[t][:], acc[t][:], -2.0, nb[:], ALU.mult, ALU.add)
+
+        def rowmin(t):
+            zmin[t] = keep.tile([P, 1], F32, name="zmin%d" % t)
+            nc.vector.tensor_reduce(zmin[t][:], z[t][:], mybir.AxisListType.X, ALU.min)
+
+        def expo(t):
+            e[t] = keep.tile([P, S], F32, name="e%d" % t)
+            ssum[t] = keep.tile([P, 1], F32, name="ssum%d" % t)
+            nc.scalar.activation(e[t][:], z[t][:], ACT.Exp, bias=zmin[t][:], scale=-1.0, accum_out=ssum[t][:])
+
+        def recip(t):
+            rinv[t] = keep.tile([P, 1], F32, name="rinv%d" % t)
+            nc.vector.reciprocal(rinv[t][:], ssum[t][:])
+
+        def scale(eng, t):
+            o[t] = keep.tile([P, S], F32, name="o%d" % t)
+            if eng == "s":
+                nc.scalar.activation(o[t][:], e[t][:], ACT.Copy, scale=rinv[t][:])
+            elif eng == "v":
+                nc.vector.tensor_scalar(o[t][:], e[t][:], rinv[t][:], None, ALU.mult)
+            elif eng == "g":
+                nc.gpsimd.tensor_scalar(o[t][:], e[t][:], rinv[t][:], 0.0, ALU.mult, ALU.add)
+
+        def store(t):
+            nc.sync.dma_start(out[t * P : (t + 1) * P, :], o[t][:])
+
+        load_offs()
+        clear()
+        warm_exp()
+        load_norm(nc.sync)
+        make_identity(nc, ident[:])
+        load_words(0)
+        load_h(0, 0, 2)
+        load_words(1)
+        load_scales(nc.sync)
+        load_h(0, 2, 2)
+        load_words(2)
+        load_h(1, 0, 2)
+        load_h(2, 0, 2)
+        load_h(1, 2, 2)
+        load_h(2, 2, 1)
+        load_h(2, 3, 1)
+        gather_norm()
+        gather_words(0)
+        spread_norm()
+        cast("s", 0, 0, 0, 256)
+        gather_scales()
+        quant(0, 0, 0, 256)
+        mm(0, 0)
+        mm(0, 1)
+        gather_words(1)
+        cast("s", 0, 2, 0, 256)
+        quant(0, 2, 0, 256)
+        mm(0, 2)
+        mm(0, 3)
+        gather_words(2)
+        cast("s", 1, 0, 0, 256)
+        quant(1, 0, 0, 256)
+        mm(1, 0)
+        mm(1, 1)
+        cast("s", 2, 0, 0, 128)
+        cast("v", 2, 0, 128, 256)
+        quant(2, 0, 0, 128)
+        mm(2, 0)
+        quant(2, 0, 128, 256)
+        mm(2, 1)
+        cast("s", 1, 2, 0, 256)
+        dist(0)
+        rowmin(0)
+        expo(0)
+        dist(1)
+        rowmin(1)
+        quant(1, 2, 0, 256)
+        mm(1, 2)
+        mm(1, 3)
+        cast("s", 2, 2, 0, 128)
+        cast("v", 2, 3, 0, 128)
+        quant(2, 2, 0, 128)
+        mm(2, 2)
+        quant(2, 3, 0, 128)
+        mm(2, 3)
+        expo(1)
+        recip(0)
+        scale("s", 0)
+        store(0)
+        dist(2)
+        rowmin(2)
+        recip(1)
+        scale("s", 1)
+        store(1)
+        expo(2)
+        dist(3)
+        rowmin(3)
+        expo(3)
+        recip(2)
+        scale("v", 2)
+        store(2)
+        recip(3)
+        scale("v", 3)
+        store(3)

@@ -41,8 +41,11 @@ def tile_picked_zcos_nca_p_kernel(tc, x_words, x_scales, hT, norm2, offs, out):
         raw, grouped, codes, scales, where = {}, {}, {}, {}, {}
         z, e, zmin, ssum, rinv, o = {}, {}, {}, {}, {}, {}
 
+        minus1 = keep.tile([P, 1], F32, name="minus1")
+
         def clear():
             nc.gpsimd.memset(swin[:].bitcast(I32), 0)
+            nc.gpsimd.memset(minus1[:], -1.0)
             nc.vector.memset(nwin[32:64, :], 0.0)
             nc.vector.memset(nwin[64:128, :], 0.0)
 
@@ -66,8 +69,8 @@ def tile_picked_zcos_nca_p_kernel(tc, x_words, x_scales, hT, norm2, offs, out):
         def load_h(a, t0, nt_):
             w = nt_ * P
             key = (a, t0)
-            raw[key] = keep.tile([P, 4, w], F32, name="raw%d_%d" % key)
-            grouped[key] = keep.tile([P, w, 4], BF16, name="grp%d_%d" % key, align_bytes=64)
+            raw[key] = keep.tile([P, 4, w], F32, name="raw%d_%d" % key, tag="raw%d_%d" % key, align_bytes=64)
+            grouped[key] = keep.tile([P, w, 4], BF16, name="grp%d_%d" % key, tag="grp%d_%d" % key, align_bytes=64)
             codes[key] = keep.tile([P, w], U32, name="cod%d_%d" % key, align_bytes=64)
             scales[key] = keep.tile([P, w], U8, name="scl%d_%d" % key, align_bytes=64)
             for t in range(nt_):
@@ -109,7 +112,7 @@ def tile_picked_zcos_nca_p_kernel(tc, x_words, x_scales, hT, norm2, offs, out):
                 nc.tensor.transpose(nbp[:, b, :], ncol[:, b : b + 1].to_broadcast([P, P]), ident[:])
             nc.scalar.copy(nb[:], nbp[:].rearrange("p b c -> p (b c)"))
 
-        def mm(a, t):
+        def mm(a, t, order=(0, 1, 2)):
             key, i = where[(a, t)]
             cols = slice(i * P, (i + 1) * P)
             nc.tensor.matmul_mx(
@@ -118,26 +121,29 @@ def tile_picked_zcos_nca_p_kernel(tc, x_words, x_scales, hT, norm2, offs, out):
                 lhsT_scale=scales[key][:, cols],
                 rhs=xw[a][:].bitcast(FP8X4),
                 rhs_scale=xs[4 * a : P, :],
-                start=(a == 0),
-                stop=(a == PASSES - 1),
+                start=(a == order[0]),
+                stop=(a == order[2]),
             )
 
-        def dist(t):
-            z[t] = keep.tile([P, S], F32, name="z%d" % t)
+        def dist(t, tag=None):
+            z[t] = keep.tile([P, S], F32, name="z%d" % t, tag=tag or "z%d" % t, align_bytes=64)
             nc.vector.scalar_tensor_tensor(z[t][:], acc[t][:], -2.0, nb[:], ALU.mult, ALU.add)
 
-        def rowmin(t):
-            zmin[t] = keep.tile([P, 1], F32, name="zmin%d" % t)
+        def rowmin(t, tag=None):
+            zmin[t] = keep.tile([P, 1], F32, name="zmin%d" % t, tag=tag or "zmin%d" % t, align_bytes=64)
             nc.vector.tensor_reduce(zmin[t][:], z[t][:], mybir.AxisListType.X, ALU.min)
 
-        def expo(t):
-            e[t] = keep.tile([P, S], F32, name="e%d" % t)
+        def expo(t, tag=None):
+            e[t] = keep.tile([P, S], F32, name="e%d" % t, tag=tag or "e%d" % t, align_bytes=64)
             ssum[t] = keep.tile([P, 1], F32, name="ssum%d" % t)
             nc.scalar.activation(e[t][:], z[t][:], ACT.Exp, bias=zmin[t][:], scale=-1.0, accum_out=ssum[t][:])
 
-        def recip(t):
+        def recip(eng, t):
             rinv[t] = keep.tile([P, 1], F32, name="rinv%d" % t)
-            nc.vector.reciprocal(rinv[t][:], ssum[t][:])
+            if eng == "v":
+                nc.vector.reciprocal(rinv[t][:], ssum[t][:])
+            else:
+                nc.gpsimd.tensor_tensor(rinv[t][:], ssum[t][:], minus1[:], ALU.pow)
 
         def scale(eng, t):
             o[t] = keep.tile([P, S], F32, name="o%d" % t)
@@ -148,6 +154,12 @@ def tile_picked_zcos_nca_p_kernel(tc, x_words, x_scales, hT, norm2, offs, out):
             elif eng == "g":
                 nc.gpsimd.tensor_scalar(o[t][:], e[t][:], rinv[t][:], 0.0, ALU.mult, ALU.add)
 
+        def finish_halves(t):
+            o[t] = keep.tile([P, S], F32, name="o%d" % t)
+            for cols, queue in ((slice(0, S // 2), nc.sync), (slice(S // 2, S), nc.scalar)):
+                nc.vector.tensor_scalar(o[t][:, cols], e[t][:, cols], rinv[t][:], None, ALU.mult)
+                queue.dma_start(out[t * P : (t + 1) * P, cols], o[t][:, cols])
+
         def store(t):
             nc.sync.dma_start(out[t * P : (t + 1) * P, :], o[t][:])
 
@@ -157,71 +169,75 @@ def tile_picked_zcos_nca_p_kernel(tc, x_words, x_scales, hT, norm2, offs, out):
         load_norm(nc.sync)
         make_identity(nc, ident[:])
         load_words(0)
-        load_h(0, 0, 2)
         load_words(1)
-        load_scales(nc.sync)
-        load_h(0, 2, 2)
         load_words(2)
+        load_h(0, 0, 2)
+        load_scales(nc.sync)
         load_h(1, 0, 2)
         load_h(2, 0, 2)
-        load_h(1, 2, 2)
+        load_h(0, 2, 2)
+        load_h(1, 2, 1)
         load_h(2, 2, 1)
+        load_h(1, 3, 1)
         load_h(2, 3, 1)
         gather_norm()
-        gather_words(0)
         spread_norm()
+        gather_words(0)
+        gather_words(1)
+        gather_words(2)
         cast("s", 0, 0, 0, 256)
         gather_scales()
         quant(0, 0, 0, 256)
         mm(0, 0)
         mm(0, 1)
-        gather_words(1)
-        cast("s", 0, 2, 0, 256)
-        quant(0, 2, 0, 256)
-        mm(0, 2)
-        mm(0, 3)
-        gather_words(2)
-        cast("s", 1, 0, 0, 256)
+        cast("v", 1, 0, 0, 128)
+        cast("s", 1, 0, 128, 256)
         quant(1, 0, 0, 256)
         mm(1, 0)
         mm(1, 1)
-        cast("s", 2, 0, 0, 128)
-        cast("v", 2, 0, 128, 256)
-        quant(2, 0, 0, 128)
+        cast("v", 2, 0, 0, 128)
+        cast("s", 2, 0, 128, 256)
+        quant(2, 0, 0, 256)
         mm(2, 0)
-        quant(2, 0, 128, 256)
         mm(2, 1)
-        cast("s", 1, 2, 0, 256)
-        dist(0)
-        rowmin(0)
-        expo(0)
-        dist(1)
-        rowmin(1)
-        quant(1, 2, 0, 256)
+        cast("v", 0, 2, 0, 128)
+        cast("s", 0, 2, 128, 256)
+        quant(0, 2, 0, 128)
+        mm(0, 2)
+        quant(0, 2, 128, 256)
+        mm(0, 3)
+        cast("s", 1, 2, 0, 128)
+        dist(0, "grp0_2")
+        quant(1, 2, 0, 128)
         mm(1, 2)
-        mm(1, 3)
         cast("s", 2, 2, 0, 128)
-        cast("v", 2, 3, 0, 128)
+        dist(1, "grp1_2")
         quant(2, 2, 0, 128)
         mm(2, 2)
+        cast("s", 1, 3, 0, 128)
+        rowmin(0, "grp2_2")
+        quant(1, 3, 0, 128)
+        mm(1, 3)
+        cast("s", 2, 3, 0, 128)
+        expo(0, "raw2_3")
+        dist(2, "grp1_3")
         quant(2, 3, 0, 128)
         mm(2, 3)
-        expo(1)
-        recip(0)
-        scale("s", 0)
+        recip("g", 0)
+        scale("g", 0)
         store(0)
-        dist(2)
+        rowmin(1, "grp2_3")
+        expo(1)
         rowmin(2)
-        recip(1)
-        scale("s", 1)
+        recip("g", 1)
+        scale("g", 1)
         store(1)
         expo(2)
         dist(3)
         rowmin(3)
         expo(3)
-        recip(2)
+        recip("v", 2)
         scale("v", 2)
         store(2)
-        recip(3)
-        scale("v", 3)
-        store(3)
+        recip("v", 3)
+        finish_halves(3)

@@ -125,8 +125,8 @@ def tile_picked_zcos_nca_p_kernel(tc, x_words, x_scales, hT, norm2, offs, out):
                 stop=(a == order[2]),
             )
 
-        def dist(t, tag=None):
-            z[t] = keep.tile([P, S], F32, name="z%d" % t, tag=tag or "z%d" % t, align_bytes=64)
+        def dist(t, into=None):
+            z[t] = into if into is not None else keep.tile([P, S], F32, name="z%d" % t, align_bytes=64)
             nc.vector.scalar_tensor_tensor(z[t][:], acc[t][:], -2.0, nb[:], ALU.mult, ALU.add)
 
         def rowmin(t, tag=None):
@@ -168,76 +168,84 @@ def tile_picked_zcos_nca_p_kernel(tc, x_words, x_scales, hT, norm2, offs, out):
         warm_exp()
         load_norm(nc.sync)
         make_identity(nc, ident[:])
-        load_words(0)
         load_words(1)
-        load_words(2)
+        load_words(0)
         load_h(0, 0, 2)
         load_scales(nc.sync)
-        load_h(1, 0, 2)
-        load_h(2, 0, 2)
-        load_h(0, 2, 2)
+        load_h(2, 0, 1)
+        load_words(2)
+        load_h(1, 0, 1)
+        load_h(1, 1, 1)
+        load_h(2, 1, 1)
         load_h(1, 2, 1)
+        load_h(0, 2, 1)
+        load_h(0, 3, 1)
         load_h(2, 2, 1)
         load_h(1, 3, 1)
         load_h(2, 3, 1)
         gather_norm()
         spread_norm()
-        gather_words(0)
         gather_words(1)
-        gather_words(2)
-        cast("s", 0, 0, 0, 256)
+        gather_words(0)
+        cast("v", 0, 0, 128, 256)
+        cast("s", 0, 0, 0, 128)
         gather_scales()
-        quant(0, 0, 0, 256)
-        mm(0, 0)
-        mm(0, 1)
-        cast("v", 1, 0, 0, 128)
-        cast("s", 1, 0, 128, 256)
-        quant(1, 0, 0, 256)
-        mm(1, 0)
-        mm(1, 1)
-        cast("v", 2, 0, 0, 128)
-        cast("s", 2, 0, 128, 256)
-        quant(2, 0, 0, 256)
-        mm(2, 0)
-        mm(2, 1)
-        cast("v", 0, 2, 0, 128)
-        cast("s", 0, 2, 128, 256)
-        quant(0, 2, 0, 128)
-        mm(0, 2)
-        quant(0, 2, 128, 256)
-        mm(0, 3)
+        cast("s", 2, 0, 0, 128)
+        quant(0, 0, 128, 256)
+        quant(0, 0, 0, 128)
+        mm(0, 1, (0, 1, 2))
+        quant(2, 0, 0, 128)
+        mm(0, 0, (0, 2, 1))
+        gather_words(2)
+        cast("s", 1, 0, 0, 128)
+        cast("s", 1, 1, 0, 128)
+        quant(1, 0, 0, 128)
+        mm(2, 0, (0, 2, 1))
+        cast("v", 2, 1, 0, 128)
         cast("s", 1, 2, 0, 128)
-        dist(0, "grp0_2")
+        quant(1, 1, 0, 128)
+        mm(1, 0, (0, 2, 1))
+        quant(2, 1, 0, 128)
+        mm(1, 1, (0, 1, 2))
+        cast("s", 0, 2, 0, 128)
         quant(1, 2, 0, 128)
-        mm(1, 2)
+        mm(2, 1, (0, 1, 2))
+        zs12 = keep.tile([P, 2, S], F32, name="zs12", tag="grp1_2", align_bytes=64)
+        dist(0, zs12[:, 0, :])
+        cast("s", 0, 3, 0, 128)
+        mm(1, 2, (1, 0, 2))
+        quant(0, 2, 0, 128)
+        dist(1, zs12[:, 1, :])
         cast("s", 2, 2, 0, 128)
-        dist(1, "grp1_2")
-        quant(2, 2, 0, 128)
-        mm(2, 2)
+        mm(0, 2, (1, 0, 2))
+        quant(0, 3, 0, 128)
         cast("s", 1, 3, 0, 128)
+        quant(2, 2, 0, 128)
         rowmin(0, "grp2_2")
-        quant(1, 3, 0, 128)
-        mm(1, 3)
+        mm(2, 2, (1, 0, 2))
         cast("s", 2, 3, 0, 128)
+        quant(1, 3, 0, 128)
+        dist(2)
         expo(0, "raw2_3")
-        dist(2, "grp1_3")
+        mm(1, 3, (1, 0, 2))
         quant(2, 3, 0, 128)
-        mm(2, 3)
+        mm(0, 3, (1, 0, 2))
         recip("g", 0)
+        rowmin(2)
+        mm(2, 3, (1, 0, 2))
         scale("g", 0)
         store(0)
         rowmin(1, "grp2_3")
-        expo(1)
-        rowmin(2)
-        recip("g", 1)
-        scale("g", 1)
-        store(1)
         expo(2)
         dist(3)
-        rowmin(3)
-        expo(3)
+        expo(1)
         recip("v", 2)
-        scale("v", 2)
+        rowmin(3)
+        scale("s", 2)
         store(2)
+        recip("v", 1)
+        scale("v", 1)
+        store(1)
+        expo(3)
         recip("v", 3)
         finish_halves(3)

@@ -170,16 +170,12 @@ def tile_picked_zcos_nca_p_kernel(tc, x_words, x_scales, hT, norm2, offs, out):
         make_identity(nc, ident[:])
         load_words(1)
         load_words(0)
-        load_h(0, 0, 2)
+        load_h(0, 0, 4)
         load_scales(nc.sync)
-        load_h(2, 0, 1)
+        load_h(1, 0, 2)
         load_words(2)
-        load_h(1, 0, 1)
-        load_h(1, 1, 1)
-        load_h(2, 1, 1)
+        load_h(2, 0, 2)
         load_h(1, 2, 1)
-        load_h(0, 2, 1)
-        load_h(0, 3, 1)
         load_h(2, 2, 1)
         load_h(1, 3, 1)
         load_h(2, 3, 1)
@@ -187,65 +183,64 @@ def tile_picked_zcos_nca_p_kernel(tc, x_words, x_scales, hT, norm2, offs, out):
         spread_norm()
         gather_words(1)
         gather_words(0)
-        cast("v", 0, 0, 128, 256)
-        cast("s", 0, 0, 0, 128)
+        cast("s", 0, 0, 128, 256)
+        cast("v", 0, 0, 0, 128)
         gather_scales()
-        cast("s", 2, 0, 0, 128)
-        quant(0, 0, 128, 256)
+        cast("s", 0, 0, 384, 512)
         quant(0, 0, 0, 128)
+        quant(0, 0, 128, 256)
+        cast("v", 0, 0, 256, 384)
+        mm(0, 0, (0, 1, 2))
         mm(0, 1, (0, 1, 2))
-        quant(2, 0, 0, 128)
-        mm(0, 0, (0, 2, 1))
-        gather_words(2)
+        quant(0, 0, 384, 512)
+        quant(0, 0, 256, 384)
         cast("s", 1, 0, 0, 128)
-        cast("s", 1, 1, 0, 128)
+        cast("s", 1, 0, 128, 256)
         quant(1, 0, 0, 128)
-        mm(2, 0, (0, 2, 1))
-        cast("v", 2, 1, 0, 128)
-        cast("s", 1, 2, 0, 128)
-        quant(1, 1, 0, 128)
-        mm(1, 0, (0, 2, 1))
-        quant(2, 1, 0, 128)
+        quant(1, 0, 128, 256)
+        mm(1, 0, (0, 1, 2))
         mm(1, 1, (0, 1, 2))
-        cast("s", 0, 2, 0, 128)
-        quant(1, 2, 0, 128)
+        gather_words(2)
+        cast("s", 2, 0, 0, 128)
+        cast("s", 2, 0, 128, 256)
+        quant(2, 0, 0, 128)
+        cast("v", 1, 2, 0, 128)
+        mm(2, 0, (0, 1, 2))
+        quant(2, 0, 128, 256)
         mm(2, 1, (0, 1, 2))
-        zs12 = keep.tile([P, 2, S], F32, name="zs12", tag="grp1_2", align_bytes=64)
-        dist(0, zs12[:, 0, :])
-        cast("s", 0, 3, 0, 128)
-        mm(1, 2, (1, 0, 2))
-        quant(0, 2, 0, 128)
-        dist(1, zs12[:, 1, :])
+        dist(0)
         cast("s", 2, 2, 0, 128)
-        mm(0, 2, (1, 0, 2))
-        quant(0, 3, 0, 128)
-        cast("s", 1, 3, 0, 128)
+        quant(1, 2, 0, 128)
+        mm(0, 2, (0, 1, 2))
+        mm(1, 2, (0, 1, 2))
+        dist(1)
         quant(2, 2, 0, 128)
-        rowmin(0, "grp2_2")
-        mm(2, 2, (1, 0, 2))
-        cast("s", 2, 3, 0, 128)
+        cast("s", 1, 3, 0, 128)
+        mm(2, 2, (0, 1, 2))
+        rowmin(0, "grp1_2")
+        mm(0, 3, (0, 1, 2))
         quant(1, 3, 0, 128)
-        dist(2)
-        expo(0, "raw2_3")
-        mm(1, 3, (1, 0, 2))
+        cast("s", 2, 3, 0, 128)
+        mm(1, 3, (0, 1, 2))
+        rowmin(1)
         quant(2, 3, 0, 128)
-        mm(0, 3, (1, 0, 2))
-        recip("g", 0)
-        rowmin(2)
-        mm(2, 3, (1, 0, 2))
-        scale("g", 0)
-        store(0)
-        rowmin(1, "grp2_3")
-        expo(2)
-        dist(3)
+        expo(0, "raw2_3")
+        mm(2, 3, (0, 1, 2))
+        dist(2)
         expo(1)
-        recip("v", 2)
-        rowmin(3)
-        scale("s", 2)
-        store(2)
-        recip("v", 1)
-        scale("v", 1)
+        recip("g", 0)
+        dist(3)
+        scale("s", 0)
+        store(0)
+        recip("g", 1)
+        rowmin(2)
+        scale("g", 1)
         store(1)
+        rowmin(3)
+        expo(2)
         expo(3)
+        recip("v", 2)
+        scale("v", 2)
+        store(2)
         recip("v", 3)
         finish_halves(3)

from contextlib import ExitStack

import concourse.mybir as mybir
from concourse.masks import make_identity

K, T, S, J = 1536, 1024, 512, 512
P = 128
PASSES = 3
F32 = mybir.dt.float32
BF16 = mybir.dt.bfloat16
U32 = mybir.dt.uint32
I32 = mybir.dt.int32
U16 = mybir.dt.uint16
U8 = mybir.dt.uint8
FP8X4 = mybir.dt.float8_e4m3fn_x4
ALU = mybir.AluOpType
ACT = mybir.ActivationFunctionType
FLOPS = 2 * K * S * J


def tile_picked_zcos_nca_p_kernel(tc, x_words, x_scales, hT, norm2, offs, out):
    nc = tc.nc
    with ExitStack() as ctx:
        keep = ctx.enter_context(tc.tile_pool(name="keep", bufs=1))
        psum = ctx.enter_context(tc.psum_pool(name="psum", bufs=1))

        offsets = keep.tile([P, S // 16], U16, name="offsets")
        nwin = keep.tile([P, T], F32, name="nwin")
        swin = keep.tile([P, T], U8, name="swin", align_bytes=64)
        wwin = [keep.tile([P, T], I32, name="wwin%d" % a, align_bytes=64) for a in range(PASSES)]
        xw = [keep.tile([P, S], U32, name="xw%d" % a, align_bytes=64) for a in range(PASSES)]
        xs = keep.tile([P, S], U8, name="xs", align_bytes=64)
        ng = keep.tile([P, S], F32, name="ng")
        ncol = keep.tile([P, 4], F32, name="ncol")
        nb = keep.tile([P, S], F32, name="nb")
        ident = keep.tile([P, P], F32, name="ident")
        warm = keep.tile([P, 2], F32, name="warm")
        acc = [psum.tile([P, S], F32, name="acc%d" % t) for t in range(4)]
        nt = psum.tile([P, 4, P], F32, name="nt")
        nbp = psum.tile([P, 4, P], F32, name="nbp")
        raw, grouped, codes, scales, where = {}, {}, {}, {}, {}
        z, e, zmin, ssum, rinv, o = {}, {}, {}, {}, {}, {}

        minus1 = keep.tile([P, 1], F32, name="minus1")

        def clear():
            nc.gpsimd.memset(swin[:].bitcast(I32), 0)
            nc.gpsimd.memset(minus1[:], -1.0)
            nc.vector.memset(nwin[32:64, :], 0.0)
            nc.vector.memset(nwin[64:128, :], 0.0)

        def warm_exp():
            nc.vector.memset(warm[:, 0:1], 0.0)
            nc.scalar.activation(warm[:, 1:2], warm[:, 0:1], ACT.Exp)

        def load_offs():
            nc.sync.dma_start(offsets[:], offs)

        def load_norm(eng):
            eng.dma_start(nwin[0:32, :], norm2[0:32, :])

        def load_scales(eng):
            for q in range(4):
                eng.dma_start(swin[32 * q : 32 * q + 12, :].bitcast(I32), x_scales[:, 4 * q : 4 * q + 4, :].bitcast(I32))

        def load_words(a):
            nc.sync.dma_start(wwin[a][:], x_words[a].rearrange("p n t -> p (n t)").bitcast(I32))

        def load_h(a, t0, nt_):
            w = nt_ * P
            key = (a, t0)
            raw[key] = keep.tile([P, 4, w], F32, name="raw%d_%d" % key, tag="raw%d_%d" % key, align_bytes=64)
            grouped[key] = keep.tile([P, w, 4], BF16, name="grp%d_%d" % key, tag="grp%d_%d" % key, align_bytes=64)
            codes[key] = keep.tile([P, w], U32, name="cod%d_%d" % key, align_bytes=64)
            scales[key] = keep.tile([P, w], U8, name="scl%d_%d" % key, align_bytes=64)
            for t in range(nt_):
                where[(a, t0 + t)] = (key, t)
            rows = hT[a * 512 : (a + 1) * 512, t0 * P : t0 * P + w]
            nc.sync.dma_start(raw[key][:], rows.rearrange("(p j) w -> p j w", j=4))

        def cast(eng, a, t0, c0, c1):
            key = (a, t0)
            dst = grouped[key][:, c0:c1, :].rearrange("p (c i) t -> p c t i", i=4)
            src = raw[key][:, :, c0:c1].rearrange("p t (c i) -> p c t i", i=4)
            if eng == "s":
                nc.scalar.copy(dst, src)
            elif eng == "v":
                nc.vector.tensor_copy(dst, src)

        def quant(a, t0, c0, c1):
            key = (a, t0)
            nc.vector.quantize_mx(
                out=codes[key][:, c0:c1].bitcast(FP8X4),
                scales=scales[key][:, c0:c1],
                in_=grouped[key][:, c0:c1, :].rearrange("p w j -> p (w j)"),
            )

        def gather_words(a):
            nc.vector.tensor_copy(xw[a][:], wwin[a][:].bitcast(U32).indirect(offsets[:]))

        def gather_scales():
            nc.vector.tensor_copy(xs[:], swin[:].indirect(offsets[:]))

        def gather_norm():
            nc.vector.tensor_copy(ng[:], nwin[:].indirect(offsets[:]))

        def spread_norm():
            for b in range(4):
                nc.tensor.transpose(nt[:, b, :], ng[:, b * P : (b + 1) * P], ident[:])
            nc.scalar.copy(ncol[:], nt[:, :, 0])
            for b in range(4):
                nc.tensor.transpose(nbp[:, b, :], ncol[:, b : b + 1].to_broadcast([P, P]), ident[:])
            nc.scalar.copy(nb[:], nbp[:].rearrange("p b c -> p (b c)"))

        def mm(a, t, order=(0, 1, 2)):
            key, i = where[(a, t)]
            cols = slice(i * P, (i + 1) * P)
            nc.tensor.matmul_mx(
                out=acc[t][:],
                lhsT=codes[key][:, cols].bitcast(FP8X4),
                lhsT_scale=scales[key][:, cols],
                rhs=xw[a][:].bitcast(FP8X4),
                rhs_scale=xs[4 * a : P, :],
                start=(a == order[0]),
                stop=(a == order[2]),
            )

        def dist(t, into=None):
            z[t] = into if into is not None else keep.tile([P, S], F32, name="z%d" % t, align_bytes=64)
            nc.vector.scalar_tensor_tensor(z[t][:], acc[t][:], -2.0, nb[:], ALU.mult, ALU.add)

        def rowmin(t, tag=None):
            zmin[t] = keep.tile([P, 1], F32, name="zmin%d" % t, tag=tag or "zmin%d" % t, align_bytes=64)
            nc.vector.tensor_reduce(zmin[t][:], z[t][:], mybir.AxisListType.X, ALU.min)

        def expo(t, tag=None):
            e[t] = keep.tile([P, S], F32, name="e%d" % t, tag=tag or "e%d" % t, align_bytes=64)
            ssum[t] = keep.tile([P, 1], F32, name="ssum%d" % t)
            nc.scalar.activation(e[t][:], z[t][:], ACT.Exp, bias=zmin[t][:], scale=-1.0, accum_out=ssum[t][:])

        def recip(eng, t):
            rinv[t] = keep.tile([P, 1], F32, name="rinv%d" % t)
            if eng == "v":
                nc.vector.reciprocal(rinv[t][:], ssum[t][:])
            else:
                nc.gpsimd.tensor_tensor(rinv[t][:], ssum[t][:], minus1[:], ALU.pow)

        def scale(eng, t):
            o[t] = keep.tile([P, S], F32, name="o%d" % t)
            if eng == "s":
                nc.scalar.activation(o[t][:], e[t][:], ACT.Copy, scale=rinv[t][:])
            elif eng == "v":
                nc.vector.tensor_scalar(o[t][:], e[t][:], rinv[t][:], None, ALU.mult)
            elif eng == "g":
                nc.gpsimd.tensor_scalar(o[t][:], e[t][:], rinv[t][:], 0.0, ALU.mult, ALU.add)

        def finish_halves(t):
            o[t] = keep.tile([P, S], F32, name="o%d" % t)
            for cols, queue in ((slice(0, S // 2), nc.sync), (slice(S // 2, S), nc.scalar)):
                nc.vector.tensor_scalar(o[t][:, cols], e[t][:, cols], rinv[t][:], None, ALU.mult)
                queue.dma_start(out[t * P : (t + 1) * P, cols], o[t][:, cols])

        def store(t):
            nc.sync.dma_start(out[t * P : (t + 1) * P, :], o[t][:])

        load_offs()
        clear()
        warm_exp()
        load_norm(nc.sync)
        make_identity(nc, ident[:])
        load_words(1)
        load_words(0)
        load_h(0, 0, 4)
        load_scales(nc.sync)
        load_h(1, 0, 2)
        load_words(2)
        load_h(2, 0, 2)
        load_h(1, 2, 1)
        load_h(2, 2, 1)
        load_h(1, 3, 1)
        load_h(2, 3, 1)
        gather_norm()
        spread_norm()
        gather_words(1)
        gather_words(0)
        cast("s", 0, 0, 128, 256)
        cast("v", 0, 0, 0, 128)
        gather_scales()
        cast("s", 0, 0, 384, 512)
        quant(0, 0, 0, 128)
        quant(0, 0, 128, 256)
        cast("v", 0, 0, 256, 384)
        mm(0, 0, (0, 1, 2))
        mm(0, 1, (0, 1, 2))
        quant(0, 0, 384, 512)
        quant(0, 0, 256, 384)
        cast("s", 1, 0, 0, 128)
        cast("s", 1, 0, 128, 256)
        quant(1, 0, 0, 128)
        quant(1, 0, 128, 256)
        mm(1, 0, (0, 1, 2))
        mm(1, 1, (0, 1, 2))
        gather_words(2)
        cast("s", 2, 0, 0, 128)
        cast("s", 2, 0, 128, 256)
        quant(2, 0, 0, 128)
        cast("v", 1, 2, 0, 128)
        mm(2, 0, (0, 1, 2))
        quant(2, 0, 128, 256)
        mm(2, 1, (0, 1, 2))
        dist(0)
        cast("s", 2, 2, 0, 128)
        quant(1, 2, 0, 128)
        mm(0, 2, (0, 1, 2))
        mm(1, 2, (0, 1, 2))
        dist(1)
        quant(2, 2, 0, 128)
        cast("s", 1, 3, 0, 128)
        mm(2, 2, (0, 1, 2))
        rowmin(0, "grp1_2")
        mm(0, 3, (0, 1, 2))
        quant(1, 3, 0, 128)
        cast("s", 2, 3, 0, 128)
        mm(1, 3, (0, 1, 2))
        rowmin(1)
        quant(2, 3, 0, 128)
        expo(0, "raw2_3")
        mm(2, 3, (0, 1, 2))
        dist(2)
        expo(1)
        recip("g", 0)
        dist(3)
        scale("s", 0)
        store(0)
        recip("g", 1)
        rowmin(2)
        scale("g", 1)
        store(1)
        rowmin(3)
        expo(2)
        expo(3)
        recip("v", 2)
        scale("v", 2)
        store(2)
        recip("v", 3)
        finish_halves(3)
